import numpy as np
CORES = [4,12,20,28,36,44,52,60,132,140,148,156,164,172,180,188]
N = 16
def setup_inputs(rng):
    return {"x": rng.standard_normal((N, 128, 1024), dtype=np.float32)}
def reference(x):
    b = 1024 // N
    blocks = x.reshape(N, 128, N, b)
    return {"y": np.ascontiguousarray(blocks.transpose(2, 1, 0, 3)).reshape(N, 128, 1024)}

@@ -1,0 +1,77 @@
+from concourse.bass import DstId, RemoteDMATransfer
+
+N = 16
+B = 64
+Q = 4 * B
+
+SCRATCH = {
+    "xs": ("sbuf", [128, N * B], "float32"),
+    "land": ("sbuf", [128, N * B], "float32"),
+}
+SEMAPHORES = ["loaded", "arrived", "sent", "stored"]
+
+
+def senders(r):
+    h, p = r // 8, r % 2
+    own, oth = 8 * h, 8 * (1 - h)
+    twin = r ^ 8
+    out = [(4, None, [d for d in range(own, own + 8) if d % 2 == p and d != r] + [twin])]
+    for k in range(2):
+        lo = own + 4 * k
+        out.append((6 + k, lo // 4, [d for d in range(lo, lo + 4) if d % 2 != p]))
+        lo = oth + 4 * k
+        out.append((2 + k, lo // 4, [d for d in range(lo, lo + 4) if d != twin]))
+    return out
+
+
+def engines(n):
+    return 4 if n <= 2 else 2
+
+
+def send_blocks(g, core, T, topo, r, dsts):
+    e = engines(len(dsts))
+    trs = []
+    for i, d in enumerate(dsts):
+        rid, pid = topo.addr(T.cores[d], core)
+        trs.append(RemoteDMATransfer(dst_ids=[DstId(rid=rid, pnc=pid)], dma_engine_mask=((1 << e) - 1) << (e * i),
+                                     remote_sem=T.sem.arrived, src=T.xs[:, d * B:(d + 1) * B], dst=T.land[:, r * B:(r + 1) * B]))
+    g.remote_dma_fused(trs, local_sem=T.sem.sent)
+    return e * len(dsts)
+
+
+def rank_program(g, core, T, topo):
+    chip0 = core - core % 8
+    r = T.rank_of(chip0 + 4)
+    if r is None:
+        return
+    mine = [s for s in senders(r) if s[0] == core % 8]
+    if not mine:
+        return
+    _, quarter, dsts = mine[0]
+
+    if quarter is not None:
+        g.wait_ge(T.sem.arrived, 4)
+        n = send_blocks(g, core, T, topo, r, dsts)
+        g.wait_ge(T.sem.sent, n)
+        return
+
+    g.sync.dma_start(T.xs[:], T.x[:]).then_inc(T.sem.loaded, 16)
+    g.scalar.dma_start(T.land[:, r * B:(r + 1) * B], T.x[:, r * B:(r + 1) * B]).then_inc(T.sem.arrived, 16)
+    g.wait_ge(T.sem.loaded, 16)
+    trs = []
+    for i, (k, q, _) in enumerate(s for s in senders(r) if s[1] is not None):
+        rid, pid = topo.addr(chip0 + k, core)
+        trs.append(RemoteDMATransfer(dst_ids=[DstId(rid=rid, pnc=pid)], dma_engine_mask=0xF << (4 * i),
+                                     remote_sem=T.sem.arrived, src=T.xs[:, q * Q:(q + 1) * Q], dst=T.xs[:, q * Q:(q + 1) * Q]))
+    g.remote_dma_fused(trs, local_sem=T.sem.sent)
+    n = 16 + send_blocks(g, core, T, topo, r, dsts)
+
+    total = 16
+    for s in range(N):
+        for _, _, ds in senders(s):
+            if r in ds:
+                total += engines(len(ds))
+    g.wait_ge(T.sem.arrived, total)
+    g.dma_start(T.y[:], T.land[:]).then_inc(T.sem.stored, 16)
+    g.wait_ge(T.sem.sent, n)
+    g.wait_ge(T.sem.stored, 16)

@@ -2,41 +2,20 @@ from concourse.bass import DstId, RemoteDMATransfer
 
 N = 16
 B = 64
-Q = 4 * B
+
+RUNS = [(6, 1, 4), (7, 12, 4), (2, 5, 4), (3, 9, 3)]
+HAND_ENGINES = 4
+SEND_ENGINES = 2
 
 SCRATCH = {
-    "xs": ("sbuf", [128, N * B], "float32"),
+    "xs": ("sbuf", [128, (N - 1) * B], "float32"),
     "land": ("sbuf", [128, N * B], "float32"),
 }
 SEMAPHORES = ["loaded", "arrived", "sent", "stored"]
 
 
-def senders(r):
-    h, p = r // 8, r % 2
-    own, oth = 8 * h, 8 * (1 - h)
-    twin = r ^ 8
-    out = [(4, None, [d for d in range(own, own + 8) if d % 2 == p and d != r] + [twin])]
-    for k in range(2):
-        lo = own + 4 * k
-        out.append((6 + k, lo // 4, [d for d in range(lo, lo + 4) if d % 2 != p]))
-        lo = oth + 4 * k
-        out.append((2 + k, lo // 4, [d for d in range(lo, lo + 4) if d != twin]))
-    return out
-
-
-def engines(n):
-    return 4 if n <= 2 else 2
-
-
-def send_blocks(g, core, T, topo, r, dsts):
-    e = engines(len(dsts))
-    trs = []
-    for i, d in enumerate(dsts):
-        rid, pid = topo.addr(T.cores[d], core)
-        trs.append(RemoteDMATransfer(dst_ids=[DstId(rid=rid, pnc=pid)], dma_engine_mask=((1 << e) - 1) << (e * i),
-                                     remote_sem=T.sem.arrived, src=T.xs[:, d * B:(d + 1) * B], dst=T.land[:, r * B:(r + 1) * B]))
-    g.remote_dma_fused(trs, local_sem=T.sem.sent)
-    return e * len(dsts)
+def cols(first, n):
+    return slice(first * B, (first + n) * B)
 
 
 def rank_program(g, core, T, topo):
@@ -44,34 +23,45 @@ def rank_program(g, core, T, topo):
     r = T.rank_of(chip0 + 4)
     if r is None:
         return
-    mine = [s for s in senders(r) if s[0] == core % 8]
-    if not mine:
+
+    if core % 8 != 4:
+        mine = [run for run in RUNS if run[0] == core % 8]
+        if not mine:
+            return
+        _, k0, n = mine[0]
+        g.wait_ge(T.sem.arrived, HAND_ENGINES)
+        trs = []
+        for i in range(n):
+            k = k0 + i
+            rid, pid = topo.addr(T.cores[(r + k) % N], core)
+            trs.append(RemoteDMATransfer(dst_ids=[DstId(rid=rid, pnc=pid)],
+                                         dma_engine_mask=((1 << SEND_ENGINES) - 1) << (SEND_ENGINES * i),
+                                         remote_sem=T.sem.arrived, src=T.xs[:, cols(k - 1, 1)], dst=T.land[:, cols(r, 1)]))
+        g.remote_dma_fused(trs, local_sem=T.sem.sent)
+        g.wait_ge(T.sem.sent, SEND_ENGINES * n)
         return
-    _, quarter, dsts = mine[0]
 
-    if quarter is not None:
-        g.wait_ge(T.sem.arrived, 4)
-        n = send_blocks(g, core, T, topo, r, dsts)
-        g.wait_ge(T.sem.sent, n)
-        return
+    loads = 0
+    if r < N - 1:
+        g.sync.dma_start(T.xs[:, cols(0, N - 1 - r)], T.x[:, cols(r + 1, N - 1 - r)]).then_inc(T.sem.loaded, 16)
+        loads += 16
+    if r > 0:
+        g.scalar.dma_start(T.xs[:, cols(N - 1 - r, r)], T.x[:, cols(0, r)]).then_inc(T.sem.loaded, 16)
+        loads += 16
+    g.sync.dma_start(T.land[:, cols(r, 1)], T.x[:, cols(r, 1)]).then_inc(T.sem.arrived, 16)
+    g.wait_ge(T.sem.loaded, loads)
 
-    g.sync.dma_start(T.xs[:], T.x[:]).then_inc(T.sem.loaded, 16)
-    g.scalar.dma_start(T.land[:, r * B:(r + 1) * B], T.x[:, r * B:(r + 1) * B]).then_inc(T.sem.arrived, 16)
-    g.wait_ge(T.sem.loaded, 16)
-    trs = []
-    for i, (k, q, _) in enumerate(s for s in senders(r) if s[1] is not None):
-        rid, pid = topo.addr(chip0 + k, core)
-        trs.append(RemoteDMATransfer(dst_ids=[DstId(rid=rid, pnc=pid)], dma_engine_mask=0xF << (4 * i),
-                                     remote_sem=T.sem.arrived, src=T.xs[:, q * Q:(q + 1) * Q], dst=T.xs[:, q * Q:(q + 1) * Q]))
-    g.remote_dma_fused(trs, local_sem=T.sem.sent)
-    n = 16 + send_blocks(g, core, T, topo, r, dsts)
+    for width in (4, 3):
+        trs = []
+        for i, (k, k0, n) in enumerate(RUNS):
+            if n == width:
+                rid, pid = topo.addr(chip0 + k, core)
+                trs.append(RemoteDMATransfer(dst_ids=[DstId(rid=rid, pnc=pid)],
+                                             dma_engine_mask=((1 << HAND_ENGINES) - 1) << (HAND_ENGINES * i),
+                                             remote_sem=T.sem.arrived, src=T.xs[:, cols(k0 - 1, n)], dst=T.xs[:, cols(k0 - 1, n)]))
+        g.remote_dma_fused(trs, local_sem=T.sem.sent)
 
-    total = 16
-    for s in range(N):
-        for _, _, ds in senders(s):
-            if r in ds:
-                total += engines(len(ds))
-    g.wait_ge(T.sem.arrived, total)
+    g.wait_ge(T.sem.arrived, 16 + SEND_ENGINES * (N - 1))
     g.dma_start(T.y[:], T.land[:]).then_inc(T.sem.stored, 16)
-    g.wait_ge(T.sem.sent, n)
+    g.wait_ge(T.sem.sent, HAND_ENGINES * len(RUNS))
     g.wait_ge(T.sem.stored, 16)

from concourse.bass import DstId, RemoteDMATransfer

N = 16
B = 64

RUNS = [(6, 1, 4), (7, 12, 4), (2, 5, 4), (3, 9, 3)]
HAND_ENGINES = 4
SEND_ENGINES = 2

SCRATCH = {
    "xs": ("sbuf", [128, (N - 1) * B], "float32"),
    "land": ("sbuf", [128, N * B], "float32"),
}
SEMAPHORES = ["loaded", "arrived", "sent", "stored"]


def cols(first, n):
    return slice(first * B, (first + n) * B)


def rank_program(g, core, T, topo):
    chip0 = core - core % 8
    r = T.rank_of(chip0 + 4)
    if r is None:
        return

    if core % 8 != 4:
        mine = [run for run in RUNS if run[0] == core % 8]
        if not mine:
            return
        _, k0, n = mine[0]
        g.wait_ge(T.sem.arrived, HAND_ENGINES)
        trs = []
        for i in range(n):
            k = k0 + i
            rid, pid = topo.addr(T.cores[(r + k) % N], core)
            trs.append(RemoteDMATransfer(dst_ids=[DstId(rid=rid, pnc=pid)],
                                         dma_engine_mask=((1 << SEND_ENGINES) - 1) << (SEND_ENGINES * i),
                                         remote_sem=T.sem.arrived, src=T.xs[:, cols(k - 1, 1)], dst=T.land[:, cols(r, 1)]))
        g.remote_dma_fused(trs, local_sem=T.sem.sent)
        g.wait_ge(T.sem.sent, SEND_ENGINES * n)
        return

    loads = 0
    if r < N - 1:
        g.sync.dma_start(T.xs[:, cols(0, N - 1 - r)], T.x[:, cols(r + 1, N - 1 - r)]).then_inc(T.sem.loaded, 16)
        loads += 16
    if r > 0:
        g.scalar.dma_start(T.xs[:, cols(N - 1 - r, r)], T.x[:, cols(0, r)]).then_inc(T.sem.loaded, 16)
        loads += 16
    g.sync.dma_start(T.land[:, cols(r, 1)], T.x[:, cols(r, 1)]).then_inc(T.sem.arrived, 16)
    g.wait_ge(T.sem.loaded, loads)

    for width in (4, 3):
        trs = []
        for i, (k, k0, n) in enumerate(RUNS):
            if n == width:
                rid, pid = topo.addr(chip0 + k, core)
                trs.append(RemoteDMATransfer(dst_ids=[DstId(rid=rid, pnc=pid)],
                                             dma_engine_mask=((1 << HAND_ENGINES) - 1) << (HAND_ENGINES * i),
                                             remote_sem=T.sem.arrived, src=T.xs[:, cols(k0 - 1, n)], dst=T.xs[:, cols(k0 - 1, n)]))
        g.remote_dma_fused(trs, local_sem=T.sem.sent)

    g.wait_ge(T.sem.arrived, 16 + SEND_ENGINES * (N - 1))
    g.dma_start(T.y[:], T.land[:]).then_inc(T.sem.stored, 16)
    g.wait_ge(T.sem.sent, HAND_ENGINES * len(RUNS))
    g.wait_ge(T.sem.stored, 16)
